import numpy as np
import ml_dtypes


def mxq(x, axis, fmt="e4m3"):
    dtype, down = {"e4m3": (ml_dtypes.float8_e4m3fn, 7), "e5m2": (ml_dtypes.float8_e5m2, 14)}[fmt]
    v = np.moveaxis(np.asarray(x, np.float32).astype(ml_dtypes.bfloat16).astype(np.float64), axis, -1)
    blocks = v.reshape(v.shape[:-1] + (-1, 32))
    amax = np.abs(blocks).max(-1, keepdims=True)
    byte = np.maximum(np.where(amax > 0, np.frexp(amax)[1] - 1 + 127, 0) - down, 1)
    scale = np.exp2(byte - 127.0)
    codes = (blocks / scale).astype(np.float32).astype(dtype).astype(np.float64)
    return np.moveaxis((codes * scale).reshape(v.shape), -1, axis)


WIDE = False


def mx_kscale(k):
    if not WIDE:
        return np.ones(k)
    levels = np.array([30, -30])
    if k % 512:
        return np.exp2(np.random.permutation(np.resize(levels, k // 32))).repeat(32)
    a = np.empty((k // 512, 16))
    for p in range(k // 512):
        a[p, :8] = np.random.permutation(np.resize(levels, 8))
        for g in range(8):
            far = levels[np.abs(levels - a[p, g]) >= 10]
            a[p, g + 8] = far[np.random.randint(len(far))]
    return np.exp2(a.ravel()).repeat(32)


def f64(x):
    return np.asarray(x).astype(np.float64)


def striped(idx):
    return np.tile(np.asarray(idx).reshape(-1, 16).T, (8, 1)).astype(np.uint16)


def unstriped(offs):
    return offs[:16].T.reshape(-1).astype(np.int64)


E2M1 = np.array([0.0, 0.5, 1.0, 1.5, 2.0, 3.0, 4.0, 6.0, -0.0, -0.5, -1.0, -1.5, -2.0, -3.0, -4.0, -6.0])


def pack_weight(w, fmt):
    k, n = w.shape
    w = f64(np.asarray(w, np.float32).astype(ml_dtypes.bfloat16)).reshape(k // 32, 32, n)
    amax = np.abs(w).max(1)
    if fmt in ("e4m3", "e5m2"):
        byte = np.frexp(amax)[1] - 1 + 127 - (7 if fmt == "e4m3" else 14)
    else:
        mant, ex = np.frexp(amax / 6.0)
        byte = np.where(mant > 0.5, ex, ex - 1) + 127
    byte = np.clip(np.where(amax > 0, byte, 1), 1, 254)
    scaled = (w * np.exp2(127.0 - byte)[:, None, :]).reshape(k, n).astype(np.float32)
    by_word = np.ascontiguousarray(scaled.reshape(k // 512, 128, 4, n).transpose(0, 1, 3, 2))
    if fmt in ("e4m3", "e5m2"):
        words = by_word.astype(ml_dtypes.float8_e4m3fn if fmt == "e4m3" else ml_dtypes.float8_e5m2).view(np.uint8)
    else:
        c = by_word.astype(ml_dtypes.float4_e2m1fn).view(np.uint8) & 0xF
        words = (c[..., 0::2] | (c[..., 1::2] << 4)).reshape(k // 512, 128, 2 * n)
    return np.ascontiguousarray(words), np.ascontiguousarray(byte.astype(np.uint8).reshape(k // 512, 16, n))


def unpack_weight(words, scales, fmt):
    g, _, n = scales.shape
    words = np.ascontiguousarray(words).reshape(g, 128, n, -1)
    if fmt in ("e4m3", "e5m2"):
        vals = words.view(ml_dtypes.float8_e4m3fn if fmt == "e4m3" else ml_dtypes.float8_e5m2).astype(np.float64)
    else:
        nib = np.empty((g, 128, n, 4), np.uint8)
        nib[..., 0::2] = words & 0xF
        nib[..., 1::2] = words >> 4
        vals = E2M1[nib]
    vals = vals * np.repeat(np.exp2(scales.astype(np.float64) - 127.0), 8, axis=1)[..., None]
    return vals.transpose(0, 1, 3, 2).reshape(g * 512, n)


K, T, J, R, O, N = 512, 1024, 256, 512, 256, 256


def setup_inputs():
    n = np.random.standard_normal
    idx = np.random.permutation(T)[:J]
    idx2 = np.random.permutation(J)[:O]
    idx3 = np.random.permutation(J)[:O]
    idx4 = np.random.permutation(O)[:O]
    idx5 = np.random.permutation(T)[:O]
    fk = mx_kscale(K)
    fr = mx_kscale(R)
    xtp = pack_weight(n((K, T)) / fk[:, None], "e2m1")
    wp = pack_weight(n((K, R)) * 1 / np.sqrt(K) * fk[:, None] * fr, "e5m2")
    w2p = pack_weight(n((K, R)) * 1 / np.sqrt(K) * fk[:, None] * fr, "e4m3")
    wbp = pack_weight(n((R, N)) * 1 / np.sqrt(R) / fr[:, None], "e4m3")
    wsp = pack_weight(n((K, N)) * 1 / np.sqrt(K) * fk[:, None], "e4m3")
    return {
        "xt_words": xtp[0],
        "xt_scales": xtp[1],
        "w_words": wp[0],
        "w_scales": wp[1],
        "w2_words": w2p[0],
        "w2_scales": w2p[1],
        "wb_words": wbp[0],
        "wb_scales": wbp[1],
        "ws_words": wsp[0],
        "ws_scales": wsp[1],
        "offs": striped(idx),
        "offs2": striped(idx2),
        "offs3": striped(idx3),
        "offs4": striped(idx4),
        "offs5": striped(idx5),
    }


def reference(xt_words, xt_scales, w_words, w_scales, w2_words, w2_scales, wb_words, wb_scales, ws_words, ws_scales, offs, offs2, offs3, offs4, offs5):
    idx = unstriped(offs)
    idx2 = unstriped(offs2)
    idx3 = unstriped(offs3)
    idx4 = unstriped(offs4)
    idx5 = unstriped(offs5)
    xtu = unpack_weight(xt_words, xt_scales, "e2m1")
    wu = unpack_weight(w_words, w_scales, "e5m2")
    w2u = unpack_weight(w2_words, w2_scales, "e4m3")
    wbu = unpack_weight(wb_words, wb_scales, "e4m3")
    wsu = unpack_weight(ws_words, ws_scales, "e4m3")
    xtidxg = xtu[:, idx]
    a = wu.T @ xtidxg
    b = w2u.T @ xtidxg
    ca = np.maximum(a[:, idx2], b[:, idx3])
    hid = np.abs(ca - ca[:, idx4])
    hidq = mxq(hid, 0, "e5m2")
    xtidx5g = xtu[:, idx5]
    y = wbu.T @ hidq + wsu.T @ xtidx5g
    return y

@@ -1,0 +1,193 @@
+from contextlib import ExitStack
+
+import concourse.mybir as mybir
+
+K, T, J, R, O, N = 512, 1024, 256, 512, 256, 256
+P = 128
+PACK = 4
+HALF = O // 2
+
+F32 = mybir.dt.float32
+BF16 = mybir.dt.bfloat16
+I32 = mybir.dt.int32
+U32 = mybir.dt.uint32
+U16 = mybir.dt.uint16
+U8 = mybir.dt.uint8
+E4M3 = mybir.dt.float8_e4m3fn_x4
+E5M2 = mybir.dt.float8_e5m2_x4
+E2M1 = mybir.dt.float4_e2m1fn_x4
+ACT = mybir.ActivationFunctionType
+ALU = mybir.AluOpType
+
+FLOPS = 2 * K * R * J * 2 + 2 * R * N * O + 2 * K * N * O
+
+
+def tile_list_pairedplaces_twow_further_plain_kernel(
+    tc, xt_words, xt_scales, w_words, w_scales, w2_words, w2_scales, wb_words, wb_scales,
+    ws_words, ws_scales, offs, offs2, offs3, offs4, offs5, out,
+):
+    nc = tc.nc
+    with ExitStack() as ctx:
+        sb = ctx.enter_context(tc.tile_pool(name="sb", bufs=1))
+        ps = ctx.enter_context(tc.psum_pool(name="ps", bufs=1))
+
+        def new(name, shape, dtype):
+            return sb.tile(shape, dtype, name=name, align_bytes=64)
+
+        def load_list(name, src):
+            tile = sb.tile([P, 16], U16, name=name)
+            nc.sync.dma_start(tile[:], src)
+            return tile
+
+        def load_words(queue, name, src, width, dtype):
+            tile = new(name, [P, width], dtype)
+            queue.dma_start(tile[:].bitcast(I32), src.bitcast(I32))
+            return tile
+
+        def load_scales(queue, name, src, width):
+            tile = new(name, [P, width], U8)
+            for q in range(4):
+                rows = src[0, 4 * q : 4 * q + 4, :].bitcast(I32)
+                queue[q % 2].dma_start(
+                    tile[32 * q : 32 * q + 32, :].bitcast(I32), rows.unsqueeze(0).broadcast_to([8, 4, width // 4])
+                )
+            return tile
+
+        def merged(words):
+            return words[0].rearrange("p n t -> p (n t)")
+
+        both = (nc.sync, nc.scalar)
+        lst1 = load_list("lst1", offs)
+        x_words = load_words(nc.scalar, "x_words", xt_words[0], T, U16)
+        x_scales = load_scales(both, "x_scales", xt_scales, T)
+        wa_raw = load_words(nc.sync, "wa_raw", merged(w_words), R, U32)
+        wb2_raw = load_words(nc.scalar, "wb2_raw", merged(w2_words), R, U32)
+        only = (nc.sync, nc.sync)
+        wa_sraw = load_scales(only, "wa_sraw", w_scales, R)
+        wb2_sraw = load_scales(only, "wb2_sraw", w2_scales, R)
+        lst5 = load_list("lst5", offs5)
+        lst2 = load_list("lst2", offs2)
+        lst3 = load_list("lst3", offs3)
+        lst4 = load_list("lst4", offs4)
+        short_words = load_words(nc.sync, "short_words", merged(ws_words), N, U32)
+        short_scales = load_scales(only, "short_scales", ws_scales, N)
+        out_words = load_words(nc.sync, "out_words", merged(wb_words), N, U32)
+        out_scales = load_scales(only, "out_scales", wb_scales, N)
+
+        def pick_tokens(name, lst):
+            words = new(name + "_words", [P, J], U16)
+            scales = new(name + "_scales", [P, J], U8)
+            nc.vector.tensor_copy(words[:], x_words[:].indirect(lst[:]))
+            nc.vector.tensor_copy(scales[:], x_scales[:].indirect(lst[:]))
+            return words, scales
+
+        def deal(engine_copy, name, raw, dtype):
+            dealt = new(name, [P, PACK, P], dtype)
+            engine_copy(
+                dealt[:].rearrange("p t (c i) -> p c t i", i=4),
+                raw[:].rearrange("p (c i t) -> p c t i", i=4, t=PACK),
+            )
+            return dealt
+
+        slot_words, slot_scales = pick_tokens("slot", lst1)
+        wa = deal(nc.scalar.copy, "wa", wa_raw, U32)
+        wa_s = deal(nc.vector.tensor_copy, "wa_s", wa_sraw, U8)
+        w2 = deal(nc.scalar.copy, "w2", wb2_raw, U32)
+        w2_s = deal(nc.vector.tensor_copy, "w2_s", wb2_sraw, U8)
+        place_words, place_scales = pick_tokens("place", lst5)
+
+        first = []
+        for t in range(PACK):
+            bank = ps.tile([P, 2 * J], F32, name="first%d" % t)
+            nc.tensor.matmul_mx(
+                out=bank[:, 0:J], lhsT=wa[:, t, :].bitcast(E5M2), lhsT_scale=wa_s[:, t, :],
+                rhs=slot_words[:].bitcast(E2M1), rhs_scale=slot_scales[:], start=True, stop=True,
+            )
+            nc.tensor.matmul_mx(
+                out=bank[:, J : 2 * J], lhsT=w2[:, t, :].bitcast(E4M3), lhsT_scale=w2_s[:, t, :],
+                rhs=slot_words[:].bitcast(E2M1), rhs_scale=slot_scales[:], start=True, stop=True,
+            )
+            first.append(bank)
+
+        result = [ps.tile([P, O], F32, name="result%d" % u) for u in range(N // P)]
+        for u in range(N // P):
+            cols = slice(u * P, (u + 1) * P)
+            nc.tensor.matmul_mx(
+                out=result[u][:], lhsT=short_words[:, cols].bitcast(E4M3), lhsT_scale=short_scales[:, cols],
+                rhs=place_words[:].bitcast(E2M1), rhs_scale=place_scales[:], start=True, stop=False,
+            )
+
+        SPARE = 96
+        ab = [new("ab%d" % t, [P, 2 * J + SPARE], F32) for t in range(PACK)]
+        keep = [new("keep%d" % t, [P, 2 * O], F32) for t in range(PACK)]
+        b_picked = [new("b_picked%d" % t, [P, O], F32) for t in range(PACK)]
+        neighbour = [new("neighbour%d" % t, [P, O], F32) for t in range(PACK)]
+        diff = [new("diff%d" % u, [P, 2, O], F32) for u in range(2)]
+        pairs = new("pairs", [P, 2, 2 * O], BF16)
+        hid = new("hid", [P, O, PACK], BF16)
+        hid_words = new("hid_words", [P, O], U32)
+        hid_scales = new("hid_scales", [P, O], U8)
+        for t in range(PACK):
+            nc.gpsimd.memset(ab[t][:, 2 * J :], 0.0)
+
+        def evacuate(t):
+            nc.scalar.copy(ab[t][:, 0 : 2 * J], first[t][:])
+
+        def pick_a(t):
+            nc.scalar.activation(keep[t][:, O:], ab[t][:, 0 : 2 * J].indirect(lst2[:]), ACT.Copy)
+
+        def pick_b(t):
+            nc.vector.tensor_copy(b_picked[t][:], ab[t][:, J:].indirect(lst3[:]))
+
+        def larger(t):
+            nc.vector.tensor_tensor(keep[t][:, 0:O], keep[t][:, O:], b_picked[t][:], ALU.max)
+
+        def pick_neighbour(t):
+            if t < 2:
+                nc.vector.tensor_copy(neighbour[t][:], keep[t][:].indirect(lst4[:]))
+            else:
+                nc.scalar.activation(neighbour[t][:], keep[t][:].indirect(lst4[:]), ACT.Copy)
+
+        def subtract(t):
+            nc.vector.tensor_tensor(diff[t // 2][:, t % 2, :], keep[t][:, 0:O], neighbour[t][:], ALU.subtract)
+
+        def magnitude(u, cols):
+            nc.scalar.activation(pairs[:, u, :].rearrange("p (o t) -> p o t", t=2)[:, cols, :], diff[u][:, :, cols].rearrange("p t o -> p o t"), ACT.Abs)
+
+        for t in range(PACK):
+            evacuate(t)
+            pick_a(t)
+            pick_b(t)
+            larger(t)
+            if t == 1:
+                pick_neighbour(0)
+        subtract(0)
+        pick_neighbour(2)
+        pick_neighbour(1)
+        pick_neighbour(3)
+        subtract(1)
+        magnitude(0, slice(0, O))
+        subtract(2)
+        subtract(3)
+        staged = [new("staged%d" % u, [P, O], F32) for u in range(N // P)]
+        for h in range(2):
+            cols = slice(h * HALF, (h + 1) * HALF)
+            magnitude(1, cols)
+            nc.vector.tensor_copy(
+                hid[:, cols, :].bitcast(I32),
+                pairs[:].bitcast(I32)[:, :, cols].rearrange("p u o -> p o u"),
+            )
+            nc.vector.quantize_mx(
+                out=hid_words[:, cols].bitcast(E5M2), scales=hid_scales[:, cols],
+                in_=hid[:, cols, :].rearrange("p o t -> p (o t)"),
+            )
+            for u in range(N // P):
+                rows = slice(u * P, (u + 1) * P)
+                nc.tensor.matmul_mx(
+                    out=result[u][:, cols], lhsT=out_words[:, rows].bitcast(E4M3), lhsT_scale=out_scales[:, rows],
+                    rhs=hid_words[:, cols].bitcast(E5M2), rhs_scale=hid_scales[:, cols], start=False, stop=(h == 1),
+                )
+        nc.scalar.copy(staged[0][:], result[0][:])
+        nc.sync.dma_start(out[0:P, :], staged[0][:])
+        nc.vector.tensor_copy(staged[1][:], result[1][:])
+        nc.scalar.dma_start(out[P : 2 * P, :], staged[1][:])

@@ -44,11 +44,11 @@ def tile_list_pairedplaces_twow_further_plain_kernel(
             queue.dma_start(tile[:].bitcast(I32), src.bitcast(I32))
             return tile
 
-        def load_scales(queue, name, src, width):
+        def load_scales(queues, name, src, width):
             tile = new(name, [P, width], U8)
             for q in range(4):
                 rows = src[0, 4 * q : 4 * q + 4, :].bitcast(I32)
-                queue[q % 2].dma_start(
+                queues[q].dma_start(
                     tile[32 * q : 32 * q + 32, :].bitcast(I32), rows.unsqueeze(0).broadcast_to([8, 4, width // 4])
                 )
             return tile
@@ -56,23 +56,22 @@ def tile_list_pairedplaces_twow_further_plain_kernel(
         def merged(words):
             return words[0].rearrange("p n t -> p (n t)")
 
-        both = (nc.sync, nc.scalar)
+        on_sync = [nc.sync] * 4
+        wa_raw = load_words(nc.gpsimd, "wa_raw", merged(w_words), R, U32)
+        wb2_raw = load_words(nc.gpsimd, "wb2_raw", merged(w2_words), R, U32)
         lst1 = load_list("lst1", offs)
         x_words = load_words(nc.scalar, "x_words", xt_words[0], T, U16)
-        x_scales = load_scales(both, "x_scales", xt_scales, T)
-        wa_raw = load_words(nc.sync, "wa_raw", merged(w_words), R, U32)
-        wb2_raw = load_words(nc.scalar, "wb2_raw", merged(w2_words), R, U32)
-        only = (nc.sync, nc.sync)
-        wa_sraw = load_scales(only, "wa_sraw", w_scales, R)
-        wb2_sraw = load_scales(only, "wb2_sraw", w2_scales, R)
+        x_scales = load_scales([nc.sync, nc.scalar, nc.sync, nc.scalar], "x_scales", xt_scales, T)
+        wa_sraw = load_scales([nc.sync, nc.scalar, nc.sync, nc.sync], "wa_sraw", w_scales, R)
+        wb2_sraw = load_scales(on_sync, "wb2_sraw", w2_scales, R)
         lst5 = load_list("lst5", offs5)
         lst2 = load_list("lst2", offs2)
         lst3 = load_list("lst3", offs3)
         lst4 = load_list("lst4", offs4)
         short_words = load_words(nc.sync, "short_words", merged(ws_words), N, U32)
-        short_scales = load_scales(only, "short_scales", ws_scales, N)
+        short_scales = load_scales(on_sync, "short_scales", ws_scales, N)
         out_words = load_words(nc.sync, "out_words", merged(wb_words), N, U32)
-        out_scales = load_scales(only, "out_scales", wb_scales, N)
+        out_scales = load_scales(on_sync, "out_scales", wb_scales, N)
 
         def pick_tokens(name, lst):
             words = new(name + "_words", [P, J], U16)
@@ -94,100 +93,125 @@ def tile_list_pairedplaces_twow_further_plain_kernel(
         wa_s = deal(nc.vector.tensor_copy, "wa_s", wa_sraw, U8)
         w2 = deal(nc.scalar.copy, "w2", wb2_raw, U32)
         w2_s = deal(nc.vector.tensor_copy, "w2_s", wb2_sraw, U8)
-        place_words, place_scales = pick_tokens("place", lst5)
 
-        first = []
-        for t in range(PACK):
-            bank = ps.tile([P, 2 * J], F32, name="first%d" % t)
+        def product(bank, stationary, stationary_scales, fmt):
             nc.tensor.matmul_mx(
-                out=bank[:, 0:J], lhsT=wa[:, t, :].bitcast(E5M2), lhsT_scale=wa_s[:, t, :],
+                out=bank, lhsT=stationary.bitcast(fmt), lhsT_scale=stationary_scales,
                 rhs=slot_words[:].bitcast(E2M1), rhs_scale=slot_scales[:], start=True, stop=True,
             )
-            nc.tensor.matmul_mx(
-                out=bank[:, J : 2 * J], lhsT=w2[:, t, :].bitcast(E4M3), lhsT_scale=w2_s[:, t, :],
-                rhs=slot_words[:].bitcast(E2M1), rhs_scale=slot_scales[:], start=True, stop=True,
-            )
-            first.append(bank)
 
-        result = [ps.tile([P, O], F32, name="result%d" % u) for u in range(N // P)]
-        for u in range(N // P):
-            cols = slice(u * P, (u + 1) * P)
-            nc.tensor.matmul_mx(
-                out=result[u][:], lhsT=short_words[:, cols].bitcast(E4M3), lhsT_scale=short_scales[:, cols],
-                rhs=place_words[:].bitcast(E2M1), rhs_scale=place_scales[:], start=True, stop=False,
-            )
+        a_bank, b_bank = [], []
+        for u in range(2):
+            bank = ps.tile([P, 2, J], F32, name="a_bank%d" % u)
+            for e in range(2):
+                product(bank[:, e, :], wa[:, 2 * u + e, :], wa_s[:, 2 * u + e, :], E5M2)
+            a_bank.append(bank)
+            bank = ps.tile([P, 2, J], F32, name="b_bank%d" % u)
+            for e in range(2):
+                product(bank[:, e, :], w2[:, 2 * u + e, :], w2_s[:, 2 * u + e, :], E4M3)
+            b_bank.append(bank)
 
-        SPARE = 96
-        ab = [new("ab%d" % t, [P, 2 * J + SPARE], F32) for t in range(PACK)]
-        keep = [new("keep%d" % t, [P, 2 * O], F32) for t in range(PACK)]
-        b_picked = [new("b_picked%d" % t, [P, O], F32) for t in range(PACK)]
-        neighbour = [new("neighbour%d" % t, [P, O], F32) for t in range(PACK)]
+        a_sb = [new("a_sb%d" % u, [P, 3 * J], F32) for u in range(2)]
+        b_sb = [new("b_sb%d" % u, [P, 3 * J], F32) for u in range(2)]
+        for u in range(2):
+            nc.vector.memset(a_sb[u][:, 2 * J :], 0.0)
+            nc.vector.memset(b_sb[u][:, 2 * J :], 0.0)
+        keep = [new("keep%d" % u, [P, 4 * O], F32) for u in range(2)]
+        b_picked = [new("b_picked%d" % u, [P, 2 * O], F32) for u in range(2)]
+        neighbour = [new("neighbour%d" % u, [P, 2, O], F32) for u in range(2)]
         diff = [new("diff%d" % u, [P, 2, O], F32) for u in range(2)]
-        pairs = new("pairs", [P, 2, 2 * O], BF16)
         hid = new("hid", [P, O, PACK], BF16)
         hid_words = new("hid_words", [P, O], U32)
         hid_scales = new("hid_scales", [P, O], U8)
-        for t in range(PACK):
-            nc.gpsimd.memset(ab[t][:, 2 * J :], 0.0)
 
-        def evacuate(t):
-            nc.scalar.copy(ab[t][:, 0 : 2 * J], first[t][:])
+        def plane(e, width=O):
+            return slice(e * O, e * O + width)
+
+        def look_up(on_scalar, dst, window, lst):
+            if on_scalar:
+                nc.scalar.activation(dst, window.indirect(lst[:]), ACT.Copy)
+            else:
+                nc.vector.tensor_copy(dst, window.indirect(lst[:]))
 
         def pick_a(t):
-            nc.scalar.activation(keep[t][:, O:], ab[t][:, 0 : 2 * J].indirect(lst2[:]), ACT.Copy)
+            look_up(True, keep[t // 2][:, plane(2 + t % 2)], a_sb[t // 2][:, plane(t % 2, 2 * J)], lst2)
 
         def pick_b(t):
-            nc.vector.tensor_copy(b_picked[t][:], ab[t][:, J:].indirect(lst3[:]))
+            look_up(False, b_picked[t // 2][:, plane(t % 2)], b_sb[t // 2][:, plane(t % 2, 2 * J)], lst3)
 
-        def larger(t):
-            nc.vector.tensor_tensor(keep[t][:, 0:O], keep[t][:, O:], b_picked[t][:], ALU.max)
+        def larger(u):
+            nc.vector.tensor_tensor(keep[u][:, 0 : 2 * O], keep[u][:, 2 * O :], b_picked[u][:], ALU.max)
 
         def pick_neighbour(t):
-            if t < 2:
-                nc.vector.tensor_copy(neighbour[t][:], keep[t][:].indirect(lst4[:]))
-            else:
-                nc.scalar.activation(neighbour[t][:], keep[t][:].indirect(lst4[:]), ACT.Copy)
+            look_up(t != 3, neighbour[t // 2][:, t % 2, :], keep[t // 2][:, plane(t % 2, 2 * O)], lst4)
 
-        def subtract(t):
-            nc.vector.tensor_tensor(diff[t // 2][:, t % 2, :], keep[t][:, 0:O], neighbour[t][:], ALU.subtract)
+        def subtract(u, planes, cols):
+            kept = keep[u][:, 0 : 2 * O].rearrange("p (e o) -> p e o", e=2)
+            nc.vector.tensor_tensor(
+                diff[u][:, planes, cols], kept[:, planes, cols], neighbour[u][:, planes, cols], ALU.subtract
+            )
 
         def magnitude(u, cols):
-            nc.scalar.activation(pairs[:, u, :].rearrange("p (o t) -> p o t", t=2)[:, cols, :], diff[u][:, :, cols].rearrange("p t o -> p o t"), ACT.Abs)
-
-        for t in range(PACK):
-            evacuate(t)
-            pick_a(t)
-            pick_b(t)
-            larger(t)
-            if t == 1:
-                pick_neighbour(0)
-        subtract(0)
-        pick_neighbour(2)
-        pick_neighbour(1)
-        pick_neighbour(3)
-        subtract(1)
-        magnitude(0, slice(0, O))
-        subtract(2)
-        subtract(3)
-        staged = [new("staged%d" % u, [P, O], F32) for u in range(N // P)]
-        for h in range(2):
-            cols = slice(h * HALF, (h + 1) * HALF)
-            magnitude(1, cols)
-            nc.vector.tensor_copy(
-                hid[:, cols, :].bitcast(I32),
-                pairs[:].bitcast(I32)[:, :, cols].rearrange("p u o -> p o u"),
+            nc.scalar.activation(
+                hid[:, cols, 2 * u : 2 * u + 2],
+                diff[u][:, :, cols].rearrange("p t o -> p o t"), ACT.Abs,
             )
+
+        def flat(bank):
+            return bank[:].rearrange("p e j -> p (e j)")
+
+        nc.scalar.copy(a_sb[0][:, 0 : 2 * J], flat(a_bank[0]))
+        nc.vector.tensor_copy(b_sb[0][:, 0 : 2 * J], flat(b_bank[0]))
+        pick_a(0)
+        pick_a(1)
+        pick_b(0)
+        pick_b(1)
+        nc.scalar.copy(a_sb[1][:, 0 : 2 * J], flat(a_bank[1]))
+        nc.scalar.copy(b_sb[1][:, 0 : 2 * J], flat(b_bank[1]))
+        larger(0)
+        pick_a(2)
+        pick_a(3)
+        pick_b(2)
+        pick_b(3)
+        larger(1)
+        every = slice(0, O)
+        halves = [slice(h * HALF, (h + 1) * HALF) for h in range(2)]
+        pick_neighbour(0)
+        pick_neighbour(1)
+        subtract(0, slice(0, 2), every)
+        pick_neighbour(3)
+        pick_neighbour(2)
+        magnitude(0, every)
+        for cols in halves:
+            subtract(1, slice(0, 2), cols)
+
+        place_words, place_scales = pick_tokens("place", lst5)
+        row_tiles = [slice(u * P, (u + 1) * P) for u in range(N // P)]
+        result = [[ps.tile([P, HALF], F32, name="result%d%d" % (h, u)) for u in range(2)] for h in range(2)]
+        for h, cols in enumerate(halves):
+            for u, rows in enumerate(row_tiles):
+                nc.tensor.matmul_mx(
+                    out=result[h][u][:], lhsT=short_words[:, rows].bitcast(E4M3), lhsT_scale=short_scales[:, rows],
+                    rhs=place_words[:, cols].bitcast(E2M1), rhs_scale=place_scales[:, cols], start=True, stop=False,
+                )
+        for cols in halves:
+            magnitude(1, cols)
+        for h, cols in enumerate(halves):
             nc.vector.quantize_mx(
                 out=hid_words[:, cols].bitcast(E5M2), scales=hid_scales[:, cols],
                 in_=hid[:, cols, :].rearrange("p o t -> p (o t)"),
             )
-            for u in range(N // P):
-                rows = slice(u * P, (u + 1) * P)
+            for u, rows in enumerate(row_tiles):
                 nc.tensor.matmul_mx(
-                    out=result[u][:, cols], lhsT=out_words[:, rows].bitcast(E4M3), lhsT_scale=out_scales[:, rows],
-                    rhs=hid_words[:, cols].bitcast(E5M2), rhs_scale=hid_scales[:, cols], start=False, stop=(h == 1),
+                    out=result[h][u][:], lhsT=out_words[:, rows].bitcast(E4M3), lhsT_scale=out_scales[:, rows],
+                    rhs=hid_words[:, cols].bitcast(E5M2), rhs_scale=hid_scales[:, cols], start=False, stop=True,
                 )
-        nc.scalar.copy(staged[0][:], result[0][:])
-        nc.sync.dma_start(out[0:P, :], staged[0][:])
-        nc.vector.tensor_copy(staged[1][:], result[1][:])
-        nc.scalar.dma_start(out[P : 2 * P, :], staged[1][:])
+        for h, cols in enumerate(halves):
+            for u, rows in enumerate(row_tiles):
+                staged = new("staged%d%d" % (h, u), [P, HALF], F32)
+                if u == 0:
+                    nc.scalar.copy(staged[:], result[h][u][:])
+                    nc.scalar.dma_start(out[rows, cols], staged[:])
+                else:
+                    nc.vector.tensor_copy(staged[:], result[h][u][:])
+                    nc.sync.dma_start(out[rows, cols], staged[:])

@@ -6,6 +6,8 @@ K, T, J, R, O, N = 512, 1024, 256, 512, 256, 256
 P = 128
 PACK = 4
 HALF = O // 2
+V_SPARE = 96
+S_SPARE = 256
 
 F32 = mybir.dt.float32
 BF16 = mybir.dt.bfloat16
@@ -57,15 +59,15 @@ def tile_list_pairedplaces_twow_further_plain_kernel(
             return words[0].rearrange("p n t -> p (n t)")
 
         on_sync = [nc.sync] * 4
-        wa_raw = load_words(nc.gpsimd, "wa_raw", merged(w_words), R, U32)
-        wb2_raw = load_words(nc.gpsimd, "wb2_raw", merged(w2_words), R, U32)
+        x_scales = load_scales([nc.sync, nc.scalar, nc.sync, nc.scalar], "x_scales", xt_scales, T)
         lst1 = load_list("lst1", offs)
         x_words = load_words(nc.scalar, "x_words", xt_words[0], T, U16)
-        x_scales = load_scales([nc.sync, nc.scalar, nc.sync, nc.scalar], "x_scales", xt_scales, T)
-        wa_sraw = load_scales([nc.sync, nc.scalar, nc.sync, nc.sync], "wa_sraw", w_scales, R)
-        wb2_sraw = load_scales(on_sync, "wb2_sraw", w2_scales, R)
+        wa_raw = load_words(nc.sync, "wa_raw", merged(w_words), R, U32)
+        wa_sraw = load_scales([nc.scalar, nc.sync, nc.sync, nc.sync], "wa_sraw", w_scales, R)
         lst5 = load_list("lst5", offs5)
+        wb2_raw = load_words(nc.sync, "wb2_raw", merged(w2_words), R, U32)
         lst2 = load_list("lst2", offs2)
+        wb2_sraw = load_scales(on_sync, "wb2_sraw", w2_scales, R)
         lst3 = load_list("lst3", offs3)
         lst4 = load_list("lst4", offs4)
         short_words = load_words(nc.sync, "short_words", merged(ws_words), N, U32)
@@ -80,19 +82,23 @@ def tile_list_pairedplaces_twow_further_plain_kernel(
             nc.vector.tensor_copy(scales[:], x_scales[:].indirect(lst[:]))
             return words, scales
 
-        def deal(engine_copy, name, raw, dtype):
-            dealt = new(name, [P, PACK, P], dtype)
+        def deal(engine_copy, dealt, raw, planes):
             engine_copy(
-                dealt[:].rearrange("p t (c i) -> p c t i", i=4),
-                raw[:].rearrange("p (c i t) -> p c t i", i=4, t=PACK),
+                dealt[:, planes, :].rearrange("p t (c i) -> p c t i", i=4),
+                raw[:].rearrange("p (c i t) -> p c t i", i=4, t=PACK)[:, :, planes, :],
             )
-            return dealt
 
         slot_words, slot_scales = pick_tokens("slot", lst1)
-        wa = deal(nc.scalar.copy, "wa", wa_raw, U32)
-        wa_s = deal(nc.vector.tensor_copy, "wa_s", wa_sraw, U8)
-        w2 = deal(nc.scalar.copy, "w2", wb2_raw, U32)
-        w2_s = deal(nc.vector.tensor_copy, "w2_s", wb2_sraw, U8)
+        wa = new("wa", [P, PACK, P], U32)
+        wa_s = new("wa_s", [P, PACK, P], U8)
+        w2 = new("w2", [P, PACK, P], U32)
+        w2_s = new("w2_s", [P, PACK, P], U8)
+        deal(nc.scalar.copy, wa, wa_raw, slice(0, 4))
+        deal(nc.vector.tensor_copy, wa_s, wa_sraw, slice(0, 2))
+        deal(nc.vector.tensor_copy, wa_s, wa_sraw, slice(2, 4))
+        place_words, place_scales = pick_tokens("place", lst5)
+        deal(nc.vector.tensor_copy, w2, wb2_raw, slice(0, 4))
+        deal(nc.gpsimd.tensor_copy, w2_s, wb2_sraw, slice(0, 4))
 
         def product(bank, stationary, stationary_scales, fmt):
             nc.tensor.matmul_mx(
@@ -100,32 +106,36 @@ def tile_list_pairedplaces_twow_further_plain_kernel(
                 rhs=slot_words[:].bitcast(E2M1), rhs_scale=slot_scales[:], start=True, stop=True,
             )
 
-        a_bank, b_bank = [], []
-        for u in range(2):
-            bank = ps.tile([P, 2, J], F32, name="a_bank%d" % u)
-            for e in range(2):
-                product(bank[:, e, :], wa[:, 2 * u + e, :], wa_s[:, 2 * u + e, :], E5M2)
-            a_bank.append(bank)
-            bank = ps.tile([P, 2, J], F32, name="b_bank%d" % u)
-            for e in range(2):
-                product(bank[:, e, :], w2[:, 2 * u + e, :], w2_s[:, 2 * u + e, :], E4M3)
-            b_bank.append(bank)
+        def first_stage(tags, words, scales, fmt):
+            banks = {}
+            for tag in tags:
+                if tag not in banks:
+                    banks[tag] = ps.tile([P, tags.count(tag) * J], F32, name=tag)
+            for t, tag in enumerate(tags):
+                e = t - tags.index(tag)
+                product(banks[tag][:, e * J : (e + 1) * J], words[:, t, :], scales[:, t, :], fmt)
+            return banks
 
-        a_sb = [new("a_sb%d" % u, [P, 3 * J], F32) for u in range(2)]
-        b_sb = [new("b_sb%d" % u, [P, 3 * J], F32) for u in range(2)]
-        for u in range(2):
-            nc.vector.memset(a_sb[u][:, 2 * J :], 0.0)
-            nc.vector.memset(b_sb[u][:, 2 * J :], 0.0)
+        a_bank = first_stage(["a0", "a1", "a23", "a23"], wa, wa_s, E5M2)
+        b_bank = first_stage(["b0", "b1", "b2", "b3"], w2, w2_s, E4M3)
+
+        a_low = new("a_low", [P, 2 * J + S_SPARE], F32)
+        a_high = new("a_high", [P, 2 * J + V_SPARE], F32)
+        nc.vector.memset(a_low[:, 2 * J :], 0.0)
+        nc.vector.memset(a_high[:, 2 * J :], 0.0)
+        b_sb = [new("b_sb%d" % u, [P, 4 * O], F32) for u in range(2)]
         keep = [new("keep%d" % u, [P, 4 * O], F32) for u in range(2)]
-        b_picked = [new("b_picked%d" % u, [P, 2 * O], F32) for u in range(2)]
         neighbour = [new("neighbour%d" % u, [P, 2, O], F32) for u in range(2)]
         diff = [new("diff%d" % u, [P, 2, O], F32) for u in range(2)]
         hid = new("hid", [P, O, PACK], BF16)
         hid_words = new("hid_words", [P, O], U32)
         hid_scales = new("hid_scales", [P, O], U8)
 
-        def plane(e, width=O):
-            return slice(e * O, e * O + width)
+        def span(first, width=O):
+            return slice(first * O, first * O + width)
+
+        def sides(tile):
+            return tile[:].rearrange("p (e s o) -> p e s o", e=2, s=2)
 
         def look_up(on_scalar, dst, window, lst):
             if on_scalar:
@@ -133,69 +143,73 @@ def tile_list_pairedplaces_twow_further_plain_kernel(
             else:
                 nc.vector.tensor_copy(dst, window.indirect(lst[:]))
 
-        def pick_a(t):
-            look_up(True, keep[t // 2][:, plane(2 + t % 2)], a_sb[t // 2][:, plane(t % 2, 2 * J)], lst2)
+        def pick_a(t, on_scalar):
+            u, e = divmod(t, 2)
+            window = (a_low, a_high)[u][:, span(e, J + (S_SPARE if on_scalar else V_SPARE))]
+            look_up(on_scalar, b_sb[u][:, span(2 * e + 1)], window, lst2)
 
-        def pick_b(t):
-            look_up(False, b_picked[t // 2][:, plane(t % 2)], b_sb[t // 2][:, plane(t % 2, 2 * J)], lst3)
+        def fetch_b(t, on_scalar):
+            u, e = divmod(t, 2)
+            copy = nc.scalar.copy if on_scalar else nc.vector.tensor_copy
+            copy(b_sb[u][:, span(2 * e)], b_bank["b%d" % t][:])
+
+        def pick_b(t, on_scalar):
+            u, e = divmod(t, 2)
+            look_up(on_scalar, keep[u][:, span(2 * e + 1)], b_sb[u][:, span(2 * e, 2 * O)], lst3)
 
         def larger(u):
-            nc.vector.tensor_tensor(keep[u][:, 0 : 2 * O], keep[u][:, 2 * O :], b_picked[u][:], ALU.max)
+            nc.vector.tensor_tensor(sides(keep[u])[:, :, 0, :], sides(b_sb[u])[:, :, 1, :], sides(keep[u])[:, :, 1, :], ALU.max)
 
-        def pick_neighbour(t):
-            look_up(t != 3, neighbour[t // 2][:, t % 2, :], keep[t // 2][:, plane(t % 2, 2 * O)], lst4)
+        def pick_neighbour(t, on_scalar):
+            u, e = divmod(t, 2)
+            look_up(on_scalar, neighbour[u][:, e, :], keep[u][:, span(2 * e, 2 * O)], lst4)
 
-        def subtract(u, planes, cols):
-            kept = keep[u][:, 0 : 2 * O].rearrange("p (e o) -> p e o", e=2)
-            nc.vector.tensor_tensor(
-                diff[u][:, planes, cols], kept[:, planes, cols], neighbour[u][:, planes, cols], ALU.subtract
-            )
+        def subtract(t):
+            u, e = divmod(t, 2)
+            nc.vector.tensor_tensor(diff[u][:, e, :], keep[u][:, span(2 * e)], neighbour[u][:, e, :], ALU.subtract)
 
-        def magnitude(u, cols):
-            nc.scalar.activation(
-                hid[:, cols, 2 * u : 2 * u + 2],
-                diff[u][:, :, cols].rearrange("p t o -> p o t"), ACT.Abs,
-            )
+        def magnitude(u, cols, on_scalar):
+            dst = hid[:, cols, 2 * u : 2 * u + 2]
+            src = diff[u][:, :, cols].rearrange("p t o -> p o t")
+            if on_scalar:
+                nc.scalar.activation(dst, src, ACT.Abs)
+            else:
+                nc.vector.scalar_tensor_tensor(dst, src, -1.0, src, ALU.mult, ALU.max)
 
-        def flat(bank):
-            return bank[:].rearrange("p e j -> p (e j)")
-
-        nc.scalar.copy(a_sb[0][:, 0 : 2 * J], flat(a_bank[0]))
-        nc.vector.tensor_copy(b_sb[0][:, 0 : 2 * J], flat(b_bank[0]))
-        pick_a(0)
-        pick_a(1)
-        pick_b(0)
-        pick_b(1)
-        nc.scalar.copy(a_sb[1][:, 0 : 2 * J], flat(a_bank[1]))
-        nc.scalar.copy(b_sb[1][:, 0 : 2 * J], flat(b_bank[1]))
-        larger(0)
-        pick_a(2)
-        pick_a(3)
-        pick_b(2)
-        pick_b(3)
-        larger(1)
         every = slice(0, O)
         halves = [slice(h * HALF, (h + 1) * HALF) for h in range(2)]
-        pick_neighbour(0)
-        pick_neighbour(1)
-        subtract(0, slice(0, 2), every)
-        pick_neighbour(3)
-        pick_neighbour(2)
-        magnitude(0, every)
-        for cols in halves:
-            subtract(1, slice(0, 2), cols)
+        nc.scalar.copy(a_low[:, span(0)], a_bank["a0"][:])
+        nc.scalar.copy(a_low[:, span(1)], a_bank["a1"][:])
+        nc.vector.tensor_copy(a_high[:, span(0, 2 * J)], a_bank["a23"][:])
+        pick_a(0, True)
+        pick_a(1, True)
+        pick_a(3, False)
+        pick_a(2, True)
+        for t in range(PACK):
+            fetch_b(t, t > 1)
+        for t in range(PACK):
+            pick_b(t, t > 1)
+        larger(0)
+        larger(1)
+        for t in range(PACK):
+            pick_neighbour(t, t != 1)
+        subtract(0)
+        subtract(1)
+        magnitude(0, every, True)
+        subtract(2)
+        subtract(3)
+        magnitude(1, halves[0], False)
+        magnitude(1, halves[1], True)
 
-        place_words, place_scales = pick_tokens("place", lst5)
         row_tiles = [slice(u * P, (u + 1) * P) for u in range(N // P)]
-        result = [[ps.tile([P, HALF], F32, name="result%d%d" % (h, u)) for u in range(2)] for h in range(2)]
+        result_tags = [["r0", "a0"], ["a1", "a23"]]
+        result = [[ps.tile([P, HALF], F32, name=result_tags[h][u]) for u in range(2)] for h in range(2)]
         for h, cols in enumerate(halves):
             for u, rows in enumerate(row_tiles):
                 nc.tensor.matmul_mx(
                     out=result[h][u][:], lhsT=short_words[:, rows].bitcast(E4M3), lhsT_scale=short_scales[:, rows],
                     rhs=place_words[:, cols].bitcast(E2M1), rhs_scale=place_scales[:, cols], start=True, stop=False,
                 )
-        for cols in halves:
-            magnitude(1, cols)
         for h, cols in enumerate(halves):
             nc.vector.quantize_mx(
                 out=hid_words[:, cols].bitcast(E5M2), scales=hid_scales[:, cols],

@@ -63,9 +63,9 @@ def tile_list_pairedplaces_twow_further_plain_kernel(
         lst1 = load_list("lst1", offs)
         x_words = load_words(nc.scalar, "x_words", xt_words[0], T, U16)
         wa_raw = load_words(nc.sync, "wa_raw", merged(w_words), R, U32)
-        wa_sraw = load_scales([nc.scalar, nc.sync, nc.sync, nc.sync], "wa_sraw", w_scales, R)
+        wb2_raw = load_words(nc.scalar, "wb2_raw", merged(w2_words), R, U32)
+        wa_sraw = load_scales(on_sync, "wa_sraw", w_scales, R)
         lst5 = load_list("lst5", offs5)
-        wb2_raw = load_words(nc.sync, "wb2_raw", merged(w2_words), R, U32)
         lst2 = load_list("lst2", offs2)
         wb2_sraw = load_scales(on_sync, "wb2_sraw", w2_scales, R)
         lst3 = load_list("lst3", offs3)
@@ -82,10 +82,10 @@ def tile_list_pairedplaces_twow_further_plain_kernel(
             nc.vector.tensor_copy(scales[:], x_scales[:].indirect(lst[:]))
             return words, scales
 
-        def deal(engine_copy, dealt, raw, planes):
+        def deal(engine_copy, dealt, raw, planes, run):
             engine_copy(
-                dealt[:, planes, :].rearrange("p t (c i) -> p c t i", i=4),
-                raw[:].rearrange("p (c i t) -> p c t i", i=4, t=PACK)[:, :, planes, :],
+                dealt[:, planes, :].rearrange("p t (c i) -> p c t i", i=run),
+                raw[:].rearrange("p (c i t) -> p c t i", i=run, t=PACK)[:, :, planes, :],
             )
 
         slot_words, slot_scales = pick_tokens("slot", lst1)
@@ -93,12 +93,13 @@ def tile_list_pairedplaces_twow_further_plain_kernel(
         wa_s = new("wa_s", [P, PACK, P], U8)
         w2 = new("w2", [P, PACK, P], U32)
         w2_s = new("w2_s", [P, PACK, P], U8)
-        deal(nc.scalar.copy, wa, wa_raw, slice(0, 4))
-        deal(nc.vector.tensor_copy, wa_s, wa_sraw, slice(0, 2))
-        deal(nc.vector.tensor_copy, wa_s, wa_sraw, slice(2, 4))
+        deal(nc.scalar.copy, wa, wa_raw, slice(0, 4), 4)
+        deal(nc.vector.tensor_copy, wa_s, wa_sraw, slice(0, 2), 16)
+        deal(nc.vector.tensor_copy, wa_s, wa_sraw, slice(2, 4), 16)
         place_words, place_scales = pick_tokens("place", lst5)
-        deal(nc.vector.tensor_copy, w2, wb2_raw, slice(0, 4))
-        deal(nc.gpsimd.tensor_copy, w2_s, wb2_sraw, slice(0, 4))
+        deal(nc.scalar.copy, w2, wb2_raw, slice(0, 4), 4)
+        deal(nc.gpsimd.tensor_copy, w2_s, wb2_sraw, slice(0, 2), 16)
+        deal(nc.gpsimd.tensor_copy, w2_s, wb2_sraw, slice(2, 4), 16)
 
         def product(bank, stationary, stationary_scales, fmt):
             nc.tensor.matmul_mx(
@@ -123,8 +124,9 @@ def tile_list_pairedplaces_twow_further_plain_kernel(
         a_high = new("a_high", [P, 2 * J + V_SPARE], F32)
         nc.vector.memset(a_low[:, 2 * J :], 0.0)
         nc.vector.memset(a_high[:, 2 * J :], 0.0)
-        b_sb = [new("b_sb%d" % u, [P, 4 * O], F32) for u in range(2)]
-        keep = [new("keep%d" % u, [P, 4 * O], F32) for u in range(2)]
+        b_sb = new("b_sb", [P, 2 * PACK * O], F32)
+        keep_low = new("keep_low", [P, 4 * O], F32)
+        b_picked_high = new("b_picked_high", [P, 2 * O], F32)
         neighbour = [new("neighbour%d" % u, [P, 2, O], F32) for u in range(2)]
         diff = [new("diff%d" % u, [P, 2, O], F32) for u in range(2)]
         hid = new("hid", [P, O, PACK], BF16)
@@ -134,8 +136,13 @@ def tile_list_pairedplaces_twow_further_plain_kernel(
         def span(first, width=O):
             return slice(first * O, first * O + width)
 
-        def sides(tile):
-            return tile[:].rearrange("p (e s o) -> p e s o", e=2, s=2)
+        def every_second(tile, first):
+            return tile[:, span(first - first % 2, 4 * O)].rearrange("p (e s o) -> p e s o", e=2, s=2)[:, :, first % 2, :]
+
+        def kept(t, width=O):
+            if t < 2:
+                return keep_low[:, span(2 * t, width)]
+            return b_sb[:, span(2 * (t - 2), width)]
 
         def look_up(on_scalar, dst, window, lst):
             if on_scalar:
@@ -146,27 +153,25 @@ def tile_list_pairedplaces_twow_further_plain_kernel(
         def pick_a(t, on_scalar):
             u, e = divmod(t, 2)
             window = (a_low, a_high)[u][:, span(e, J + (S_SPARE if on_scalar else V_SPARE))]
-            look_up(on_scalar, b_sb[u][:, span(2 * e + 1)], window, lst2)
+            look_up(on_scalar, b_sb[:, span(2 * t + 1)], window, lst2)
 
         def fetch_b(t, on_scalar):
-            u, e = divmod(t, 2)
             copy = nc.scalar.copy if on_scalar else nc.vector.tensor_copy
-            copy(b_sb[u][:, span(2 * e)], b_bank["b%d" % t][:])
+            copy(b_sb[:, span(2 * t)], b_bank["b%d" % t][:])
 
         def pick_b(t, on_scalar):
-            u, e = divmod(t, 2)
-            look_up(on_scalar, keep[u][:, span(2 * e + 1)], b_sb[u][:, span(2 * e, 2 * O)], lst3)
+            dst = keep_low[:, span(2 * t + 1)] if t < 2 else b_picked_high[:, span(t - 2)]
+            look_up(on_scalar, dst, b_sb[:, span(2 * t, 2 * O)], lst3)
 
-        def larger(u):
-            nc.vector.tensor_tensor(sides(keep[u])[:, :, 0, :], sides(b_sb[u])[:, :, 1, :], sides(keep[u])[:, :, 1, :], ALU.max)
+        def larger(dst, a_picked, b_picked):
+            nc.vector.tensor_tensor(dst, a_picked, b_picked, ALU.max)
 
         def pick_neighbour(t, on_scalar):
-            u, e = divmod(t, 2)
-            look_up(on_scalar, neighbour[u][:, e, :], keep[u][:, span(2 * e, 2 * O)], lst4)
+            look_up(on_scalar, neighbour[t // 2][:, t % 2, :], kept(t, 2 * O), lst4)
 
         def subtract(t):
             u, e = divmod(t, 2)
-            nc.vector.tensor_tensor(diff[u][:, e, :], keep[u][:, span(2 * e)], neighbour[u][:, e, :], ALU.subtract)
+            nc.vector.tensor_tensor(diff[u][:, e, :], kept(t), neighbour[u][:, e, :], ALU.subtract)
 
         def magnitude(u, cols, on_scalar):
             dst = hid[:, cols, 2 * u : 2 * u + 2]
@@ -183,14 +188,14 @@ def tile_list_pairedplaces_twow_further_plain_kernel(
         nc.vector.tensor_copy(a_high[:, span(0, 2 * J)], a_bank["a23"][:])
         pick_a(0, True)
         pick_a(1, True)
-        pick_a(3, False)
         pick_a(2, True)
+        pick_a(3, False)
         for t in range(PACK):
             fetch_b(t, t > 1)
         for t in range(PACK):
             pick_b(t, t > 1)
-        larger(0)
-        larger(1)
+        larger(every_second(keep_low, 0), every_second(b_sb, 1), every_second(keep_low, 1))
+        larger(every_second(b_sb, 0), every_second(b_sb, 5), b_picked_high[:].rearrange("p (e o) -> p e o", e=2))
         for t in range(PACK):
             pick_neighbour(t, t != 1)
         subtract(0)
@@ -202,7 +207,7 @@ def tile_list_pairedplaces_twow_further_plain_kernel(
         magnitude(1, halves[1], True)
 
         row_tiles = [slice(u * P, (u + 1) * P) for u in range(N // P)]
-        result_tags = [["r0", "a0"], ["a1", "a23"]]
+        result_tags = [["b0", "b1"], ["b2", "b3"]]
         result = [[ps.tile([P, HALF], F32, name=result_tags[h][u]) for u in range(2)] for h in range(2)]
         for h, cols in enumerate(halves):
             for u, rows in enumerate(row_tiles):
@@ -225,7 +230,7 @@ def tile_list_pairedplaces_twow_further_plain_kernel(
                 staged = new("staged%d%d" % (h, u), [P, HALF], F32)
                 if u == 0:
                     nc.scalar.copy(staged[:], result[h][u][:])
-                    nc.scalar.dma_start(out[rows, cols], staged[:])
+                    (nc.sync, nc.scalar)[h].dma_start(out[rows, cols], staged[:])
                 else:
                     nc.vector.tensor_copy(staged[:], result[h][u][:])
                     nc.sync.dma_start(out[rows, cols], staged[:])

@@ -63,9 +63,9 @@ def tile_list_pairedplaces_twow_further_plain_kernel(
         lst1 = load_list("lst1", offs)
         x_words = load_words(nc.scalar, "x_words", xt_words[0], T, U16)
         wa_raw = load_words(nc.sync, "wa_raw", merged(w_words), R, U32)
-        wb2_raw = load_words(nc.scalar, "wb2_raw", merged(w2_words), R, U32)
-        wa_sraw = load_scales(on_sync, "wa_sraw", w_scales, R)
+        wa_sraw = load_scales([nc.scalar, nc.sync, nc.sync, nc.sync], "wa_sraw", w_scales, R)
         lst5 = load_list("lst5", offs5)
+        wb2_raw = load_words(nc.sync, "wb2_raw", merged(w2_words), R, U32)
         lst2 = load_list("lst2", offs2)
         wb2_sraw = load_scales(on_sync, "wb2_sraw", w2_scales, R)
         lst3 = load_list("lst3", offs3)
@@ -97,7 +97,7 @@ def tile_list_pairedplaces_twow_further_plain_kernel(
         deal(nc.vector.tensor_copy, wa_s, wa_sraw, slice(0, 2), 16)
         deal(nc.vector.tensor_copy, wa_s, wa_sraw, slice(2, 4), 16)
         place_words, place_scales = pick_tokens("place", lst5)
-        deal(nc.scalar.copy, w2, wb2_raw, slice(0, 4), 4)
+        deal(nc.vector.tensor_copy, w2, wb2_raw, slice(0, 4), 4)
         deal(nc.gpsimd.tensor_copy, w2_s, wb2_sraw, slice(0, 2), 16)
         deal(nc.gpsimd.tensor_copy, w2_s, wb2_sraw, slice(2, 4), 16)
 
@@ -129,6 +129,7 @@ def tile_list_pairedplaces_twow_further_plain_kernel(
         b_picked_high = new("b_picked_high", [P, 2 * O], F32)
         neighbour = [new("neighbour%d" % u, [P, 2, O], F32) for u in range(2)]
         diff = [new("diff%d" % u, [P, 2, O], F32) for u in range(2)]
+        pairs = new("pairs", [P, 2, 2 * O], BF16)
         hid = new("hid", [P, O, PACK], BF16)
         hid_words = new("hid_words", [P, O], U32)
         hid_scales = new("hid_scales", [P, O], U8)
@@ -174,7 +175,7 @@ def tile_list_pairedplaces_twow_further_plain_kernel(
             nc.vector.tensor_tensor(diff[u][:, e, :], kept(t), neighbour[u][:, e, :], ALU.subtract)
 
         def magnitude(u, cols, on_scalar):
-            dst = hid[:, cols, 2 * u : 2 * u + 2]
+            dst = pairs[:, u, :].rearrange("p (o t) -> p o t", t=2)[:, cols, :]
             src = diff[u][:, :, cols].rearrange("p t o -> p o t")
             if on_scalar:
                 nc.scalar.activation(dst, src, ACT.Abs)
@@ -215,6 +216,11 @@ def tile_list_pairedplaces_twow_further_plain_kernel(
                     out=result[h][u][:], lhsT=short_words[:, rows].bitcast(E4M3), lhsT_scale=short_scales[:, rows],
                     rhs=place_words[:, cols].bitcast(E2M1), rhs_scale=place_scales[:, cols], start=True, stop=False,
                 )
+        for cols in halves:
+            nc.vector.tensor_copy(
+                hid[:, cols, :].bitcast(I32),
+                pairs[:].bitcast(I32)[:, :, cols].rearrange("p u o -> p o u"),
+            )
         for h, cols in enumerate(halves):
             nc.vector.quantize_mx(
                 out=hid_words[:, cols].bitcast(E5M2), scales=hid_scales[:, cols],

from contextlib import ExitStack

import concourse.mybir as mybir

K, T, J, R, O, N = 512, 1024, 256, 512, 256, 256
P = 128
PACK = 4
HALF = O // 2
V_SPARE = 96
S_SPARE = 256

F32 = mybir.dt.float32
BF16 = mybir.dt.bfloat16
I32 = mybir.dt.int32
U32 = mybir.dt.uint32
U16 = mybir.dt.uint16
U8 = mybir.dt.uint8
E4M3 = mybir.dt.float8_e4m3fn_x4
E5M2 = mybir.dt.float8_e5m2_x4
E2M1 = mybir.dt.float4_e2m1fn_x4
ACT = mybir.ActivationFunctionType
ALU = mybir.AluOpType

FLOPS = 2 * K * R * J * 2 + 2 * R * N * O + 2 * K * N * O


def tile_list_pairedplaces_twow_further_plain_kernel(
    tc, xt_words, xt_scales, w_words, w_scales, w2_words, w2_scales, wb_words, wb_scales,
    ws_words, ws_scales, offs, offs2, offs3, offs4, offs5, out,
):
    nc = tc.nc
    with ExitStack() as ctx:
        sb = ctx.enter_context(tc.tile_pool(name="sb", bufs=1))
        ps = ctx.enter_context(tc.psum_pool(name="ps", bufs=1))

        def new(name, shape, dtype):
            return sb.tile(shape, dtype, name=name, align_bytes=64)

        def load_list(name, src):
            tile = sb.tile([P, 16], U16, name=name)
            nc.sync.dma_start(tile[:], src)
            return tile

        def load_words(queue, name, src, width, dtype):
            tile = new(name, [P, width], dtype)
            queue.dma_start(tile[:].bitcast(I32), src.bitcast(I32))
            return tile

        def load_scales(queues, name, src, width):
            tile = new(name, [P, width], U8)
            for q in range(4):
                rows = src[0, 4 * q : 4 * q + 4, :].bitcast(I32)
                queues[q].dma_start(
                    tile[32 * q : 32 * q + 32, :].bitcast(I32), rows.unsqueeze(0).broadcast_to([8, 4, width // 4])
                )
            return tile

        def merged(words):
            return words[0].rearrange("p n t -> p (n t)")

        on_sync = [nc.sync] * 4
        x_scales = load_scales([nc.sync, nc.scalar, nc.sync, nc.scalar], "x_scales", xt_scales, T)
        lst1 = load_list("lst1", offs)
        x_words = load_words(nc.scalar, "x_words", xt_words[0], T, U16)
        wa_raw = load_words(nc.sync, "wa_raw", merged(w_words), R, U32)
        wa_sraw = load_scales([nc.scalar, nc.sync, nc.sync, nc.sync], "wa_sraw", w_scales, R)
        lst5 = load_list("lst5", offs5)
        wb2_raw = load_words(nc.sync, "wb2_raw", merged(w2_words), R, U32)
        lst2 = load_list("lst2", offs2)
        wb2_sraw = load_scales(on_sync, "wb2_sraw", w2_scales, R)
        lst3 = load_list("lst3", offs3)
        lst4 = load_list("lst4", offs4)
        short_words = load_words(nc.sync, "short_words", merged(ws_words), N, U32)
        short_scales = load_scales(on_sync, "short_scales", ws_scales, N)
        out_words = load_words(nc.sync, "out_words", merged(wb_words), N, U32)
        out_scales = load_scales(on_sync, "out_scales", wb_scales, N)

        def pick_tokens(name, lst):
            words = new(name + "_words", [P, J], U16)
            scales = new(name + "_scales", [P, J], U8)
            nc.vector.tensor_copy(words[:], x_words[:].indirect(lst[:]))
            nc.vector.tensor_copy(scales[:], x_scales[:].indirect(lst[:]))
            return words, scales

        def deal(engine_copy, dealt, raw, planes, run):
            engine_copy(
                dealt[:, planes, :].rearrange("p t (c i) -> p c t i", i=run),
                raw[:].rearrange("p (c i t) -> p c t i", i=run, t=PACK)[:, :, planes, :],
            )

        slot_words, slot_scales = pick_tokens("slot", lst1)
        wa = new("wa", [P, PACK, P], U32)
        wa_s = new("wa_s", [P, PACK, P], U8)
        w2 = new("w2", [P, PACK, P], U32)
        w2_s = new("w2_s", [P, PACK, P], U8)
        deal(nc.scalar.copy, wa, wa_raw, slice(0, 4), 4)
        deal(nc.vector.tensor_copy, wa_s, wa_sraw, slice(0, 2), 16)
        deal(nc.vector.tensor_copy, wa_s, wa_sraw, slice(2, 4), 16)
        place_words, place_scales = pick_tokens("place", lst5)
        deal(nc.vector.tensor_copy, w2, wb2_raw, slice(0, 4), 4)
        deal(nc.gpsimd.tensor_copy, w2_s, wb2_sraw, slice(0, 2), 16)
        deal(nc.gpsimd.tensor_copy, w2_s, wb2_sraw, slice(2, 4), 16)

        def product(bank, stationary, stationary_scales, fmt):
            nc.tensor.matmul_mx(
                out=bank, lhsT=stationary.bitcast(fmt), lhsT_scale=stationary_scales,
                rhs=slot_words[:].bitcast(E2M1), rhs_scale=slot_scales[:], start=True, stop=True,
            )

        def first_stage(tags, words, scales, fmt):
            banks = {}
            for tag in tags:
                if tag not in banks:
                    banks[tag] = ps.tile([P, tags.count(tag) * J], F32, name=tag)
            for t, tag in enumerate(tags):
                e = t - tags.index(tag)
                product(banks[tag][:, e * J : (e + 1) * J], words[:, t, :], scales[:, t, :], fmt)
            return banks

        a_bank = first_stage(["a0", "a1", "a23", "a23"], wa, wa_s, E5M2)
        b_bank = first_stage(["b0", "b1", "b2", "b3"], w2, w2_s, E4M3)

        a_low = new("a_low", [P, 2 * J + S_SPARE], F32)
        a_high = new("a_high", [P, 2 * J + V_SPARE], F32)
        nc.vector.memset(a_low[:, 2 * J :], 0.0)
        nc.vector.memset(a_high[:, 2 * J :], 0.0)
        b_sb = new("b_sb", [P, 2 * PACK * O], F32)
        keep_low = new("keep_low", [P, 4 * O], F32)
        b_picked_high = new("b_picked_high", [P, 2 * O], F32)
        neighbour = [new("neighbour%d" % u, [P, 2, O], F32) for u in range(2)]
        diff = [new("diff%d" % u, [P, 2, O], F32) for u in range(2)]
        pairs = new("pairs", [P, 2, 2 * O], BF16)
        hid = new("hid", [P, O, PACK], BF16)
        hid_words = new("hid_words", [P, O], U32)
        hid_scales = new("hid_scales", [P, O], U8)

        def span(first, width=O):
            return slice(first * O, first * O + width)

        def every_second(tile, first):
            return tile[:, span(first - first % 2, 4 * O)].rearrange("p (e s o) -> p e s o", e=2, s=2)[:, :, first % 2, :]

        def kept(t, width=O):
            if t < 2:
                return keep_low[:, span(2 * t, width)]
            return b_sb[:, span(2 * (t - 2), width)]

        def look_up(on_scalar, dst, window, lst):
            if on_scalar:
                nc.scalar.activation(dst, window.indirect(lst[:]), ACT.Copy)
            else:
                nc.vector.tensor_copy(dst, window.indirect(lst[:]))

        def pick_a(t, on_scalar):
            u, e = divmod(t, 2)
            window = (a_low, a_high)[u][:, span(e, J + (S_SPARE if on_scalar else V_SPARE))]
            look_up(on_scalar, b_sb[:, span(2 * t + 1)], window, lst2)

        def fetch_b(t, on_scalar):
            copy = nc.scalar.copy if on_scalar else nc.vector.tensor_copy
            copy(b_sb[:, span(2 * t)], b_bank["b%d" % t][:])

        def pick_b(t, on_scalar):
            dst = keep_low[:, span(2 * t + 1)] if t < 2 else b_picked_high[:, span(t - 2)]
            look_up(on_scalar, dst, b_sb[:, span(2 * t, 2 * O)], lst3)

        def larger(dst, a_picked, b_picked):
            nc.vector.tensor_tensor(dst, a_picked, b_picked, ALU.max)

        def pick_neighbour(t, on_scalar):
            look_up(on_scalar, neighbour[t // 2][:, t % 2, :], kept(t, 2 * O), lst4)

        def subtract(t):
            u, e = divmod(t, 2)
            nc.vector.tensor_tensor(diff[u][:, e, :], kept(t), neighbour[u][:, e, :], ALU.subtract)

        def magnitude(u, cols, on_scalar):
            dst = pairs[:, u, :].rearrange("p (o t) -> p o t", t=2)[:, cols, :]
            src = diff[u][:, :, cols].rearrange("p t o -> p o t")
            if on_scalar:
                nc.scalar.activation(dst, src, ACT.Abs)
            else:
                nc.vector.scalar_tensor_tensor(dst, src, -1.0, src, ALU.mult, ALU.max)

        every = slice(0, O)
        halves = [slice(h * HALF, (h + 1) * HALF) for h in range(2)]
        nc.scalar.copy(a_low[:, span(0)], a_bank["a0"][:])
        nc.scalar.copy(a_low[:, span(1)], a_bank["a1"][:])
        nc.vector.tensor_copy(a_high[:, span(0, 2 * J)], a_bank["a23"][:])
        pick_a(0, True)
        pick_a(1, True)
        pick_a(2, True)
        pick_a(3, False)
        for t in range(PACK):
            fetch_b(t, t > 1)
        for t in range(PACK):
            pick_b(t, t > 1)
        larger(every_second(keep_low, 0), every_second(b_sb, 1), every_second(keep_low, 1))
        larger(every_second(b_sb, 0), every_second(b_sb, 5), b_picked_high[:].rearrange("p (e o) -> p e o", e=2))
        for t in range(PACK):
            pick_neighbour(t, t != 1)
        subtract(0)
        subtract(1)
        magnitude(0, every, True)
        subtract(2)
        subtract(3)
        magnitude(1, halves[0], False)
        magnitude(1, halves[1], True)

        row_tiles = [slice(u * P, (u + 1) * P) for u in range(N // P)]
        result_tags = [["b0", "b1"], ["b2", "b3"]]
        result = [[ps.tile([P, HALF], F32, name=result_tags[h][u]) for u in range(2)] for h in range(2)]
        for h, cols in enumerate(halves):
            for u, rows in enumerate(row_tiles):
                nc.tensor.matmul_mx(
                    out=result[h][u][:], lhsT=short_words[:, rows].bitcast(E4M3), lhsT_scale=short_scales[:, rows],
                    rhs=place_words[:, cols].bitcast(E2M1), rhs_scale=place_scales[:, cols], start=True, stop=False,
                )
        for cols in halves:
            nc.vector.tensor_copy(
                hid[:, cols, :].bitcast(I32),
                pairs[:].bitcast(I32)[:, :, cols].rearrange("p u o -> p o u"),
            )
        for h, cols in enumerate(halves):
            nc.vector.quantize_mx(
                out=hid_words[:, cols].bitcast(E5M2), scales=hid_scales[:, cols],
                in_=hid[:, cols, :].rearrange("p o t -> p (o t)"),
            )
            for u, rows in enumerate(row_tiles):
                nc.tensor.matmul_mx(
                    out=result[h][u][:], lhsT=out_words[:, rows].bitcast(E4M3), lhsT_scale=out_scales[:, rows],
                    rhs=hid_words[:, cols].bitcast(E5M2), rhs_scale=hid_scales[:, cols], start=False, stop=True,
                )
        for h, cols in enumerate(halves):
            for u, rows in enumerate(row_tiles):
                staged = new("staged%d%d" % (h, u), [P, HALF], F32)
                if u == 0:
                    nc.scalar.copy(staged[:], result[h][u][:])
                    (nc.sync, nc.scalar)[h].dma_start(out[rows, cols], staged[:])
                else:
                    nc.vector.tensor_copy(staged[:], result[h][u][:])
                    nc.sync.dma_start(out[rows, cols], staged[:])
